import numpy as np
import ml_dtypes


def mxq(x, axis, fmt="e4m3"):
    dtype, down = {"e4m3": (ml_dtypes.float8_e4m3fn, 7), "e5m2": (ml_dtypes.float8_e5m2, 14)}[fmt]
    v = np.moveaxis(np.asarray(x, np.float32).astype(ml_dtypes.bfloat16).astype(np.float64), axis, -1)
    blocks = v.reshape(v.shape[:-1] + (-1, 32))
    amax = np.abs(blocks).max(-1, keepdims=True)
    byte = np.maximum(np.where(amax > 0, np.frexp(amax)[1] - 1 + 127, 0) - down, 1)
    scale = np.exp2(byte - 127.0)
    codes = (blocks / scale).astype(np.float32).astype(dtype).astype(np.float64)
    return np.moveaxis((codes * scale).reshape(v.shape), -1, axis)


WIDE = False


def mx_kscale(k):
    if not WIDE:
        return np.ones(k)
    levels = np.array([10, -10, 5, -5, 0])
    if k % 512:
        return np.exp2(np.random.permutation(np.resize(levels, k // 32))).repeat(32)
    a = np.empty((k // 512, 16))
    for p in range(k // 512):
        a[p, :8] = np.random.permutation(np.resize(levels, 8))
        for g in range(8):
            far = levels[np.abs(levels - a[p, g]) >= 10]
            a[p, g + 8] = far[np.random.randint(len(far))]
    return np.exp2(a.ravel()).repeat(32)


def f64(x):
    return np.asarray(x).astype(np.float64)


def striped(idx):
    return np.tile(idx.reshape(-1, 16).T, (8, 1)).astype(np.uint16)


def unstriped(offs):
    return offs[:16].T.reshape(-1).astype(np.int64)


def pack_weight(w):
    k, n = w.shape
    w = f64(np.asarray(w, np.float32).astype(ml_dtypes.bfloat16)).reshape(k // 32, 32, n)
    amax = np.abs(w).max(1)
    byte = np.clip(np.where(amax > 0, np.frexp(amax)[1] - 1 + 127 - 7, 1), 1, 254)
    scaled = (w * np.exp2(127.0 - byte)[:, None, :]).reshape(k, n).astype(np.float32)
    words = np.ascontiguousarray(scaled.reshape(k // 512, 128, 4, n).transpose(0, 1, 3, 2)).astype(ml_dtypes.float8_e4m3fn).view(np.uint8)
    return words, np.ascontiguousarray(byte.astype(np.uint8).reshape(k // 512, 16, n))


def unpack_weight(words, scales):
    g, p, n, _ = words.shape
    vals = np.ascontiguousarray(words).view(ml_dtypes.float8_e4m3fn).astype(np.float64) * np.repeat(np.exp2(scales.astype(np.float64) - 127.0), 8, axis=1)[..., None]
    return vals.transpose(0, 1, 3, 2).reshape(g * 512, n)


def sigmoid(v):
    return 1.0 / (1.0 + np.exp(-np.maximum(v, -700.0)))


K, T, S, D, N, U = 1024, 2048, 512, 4, 128, 1024


def setup_inputs():
    n = np.random.standard_normal
    s = mx_kscale(K)[:, None]
    packed_xT = pack_weight(n((K, T)) * s)
    return {
        "x_words": packed_xT[0],
        "x_scales": packed_xT[1],
        "w1": (n((K, N)) / np.sqrt(K) / s).astype(np.float32),
        "w2": (n((K, N)) / np.sqrt(K) / s).astype(np.float32),
        "pol": (0.3 * n((N, U))).astype(np.float32),
        "res": (np.random.uniform(0.05, 0.3, (N, 1))).astype(np.float32),
        "offs": striped(np.random.permutation(T)[:S]),
        "cel": striped(np.random.permutation(U)[:S]),
    }


def reference(x_words, x_scales, w1, w2, pol, res, offs, cel):
    xq = unpack_weight(x_words, x_scales)[:, unstriped(offs)]
    yq = mxq(f64(w1), 0, "e4m3").T @ xq
    soc = 0.9 * sigmoid(yq) + 0.05
    ocv = 0.8 * soc + 0.1 * np.log(soc) - (0.08 * np.log(-1.0 * soc + 1.0))
    yi = mxq(f64(w2), 0, "e4m3").T @ xq
    polg = f64(pol)[:, unstriped(cel)]
    pnew = 0.8 * polg + 0.1 * yi
    vt = ocv + 3.2 - (f64(res) * yi) - pnew
    return vt.reshape(len(vt), -1, D).min(axis=2) - (0.4 * (soc.reshape(len(soc), -1, D).max(axis=2)) + 2.8)

@@ -1,0 +1,139 @@
+from contextlib import ExitStack
+
+import concourse.mybir as mybir
+
+K, T, S, D, N, U = 1024, 2048, 512, 4, 128, 1024
+FLOPS = 2 * 2 * K * N * S
+
+F32 = mybir.dt.float32
+BF16 = mybir.dt.bfloat16
+I32 = mybir.dt.int32
+U32 = mybir.dt.uint32
+U16 = mybir.dt.uint16
+U8 = mybir.dt.uint8
+FP8X4 = mybir.dt.float8_e4m3fn_x4
+ALU = mybir.AluOpType
+ACT = mybir.ActivationFunctionType
+AX = mybir.AxisListType
+
+P = 128
+PACK = 4
+PASSES = K // (P * PACK)
+HALF = S // 2
+LIST_COLS = S // 16
+
+
+def tile_picked_ybatte_low_p_kernel(tc, x_words, x_scales, w1, w2, pol, res, offs, cel, out):
+    nc = tc.nc
+    with ExitStack() as ctx:
+        keep = ctx.enter_context(tc.tile_pool(name="keep", bufs=1))
+        psum = ctx.enter_context(tc.psum_pool(name="psum", bufs=1))
+
+        offs_sb = keep.tile([P, LIST_COLS], U16, name="offs_sb")
+        cel_sb = keep.tile([P, LIST_COLS], U16, name="cel_sb")
+        words = [keep.tile([P, T], U32, name=f"words{o}", tag=f"words{o}", align_bytes=64) for o in range(PASSES)]
+        planes = keep.tile([P, T], U8, name="planes", align_bytes=64)
+        w_raw = [keep.tile([P, PASSES, PACK, N], F32, name=f"w_raw{i}") for i in range(2)]
+        pol_sb = keep.tile([P, U], F32, name="pol_sb", align_bytes=64)
+        res_sb = keep.tile([P, 1], F32, name="res_sb")
+
+        def load_w(i, w):
+            nc.sync.dma_start(out=w_raw[i][:], in_=w.rearrange("(o p j) m -> p o j m", o=PASSES, j=PACK))
+
+        def load_words(o):
+            nc.sync.dma_start(out=words[o][:].bitcast(I32), in_=x_words[o].rearrange("p n t -> p (n t)").bitcast(I32))
+
+        nc.vector.memset(planes[:].bitcast(I32), 0)
+        for q in range(4):
+            nc.gpsimd.dma_start(
+                out=planes[32 * q : 32 * q + 4 * PASSES, :].bitcast(I32),
+                in_=x_scales[:, 4 * q : 4 * q + 4, :].bitcast(I32),
+            )
+        nc.scalar.dma_start(out=res_sb[:], in_=res)
+
+        load_w(0, w1)
+        nc.sync.dma_start(offs_sb[:], offs)
+        load_words(0)
+        load_w(1, w2)
+        load_words(1)
+        nc.sync.dma_start(cel_sb[:], cel)
+        nc.sync.dma_start(out=pol_sb[:], in_=pol)
+
+        w_codes, w_scales = [], []
+
+        def quantize_w(i):
+            grouped = keep.tile([P, PASSES, N, PACK], BF16, name=f"grouped{i}", align_bytes=64)
+            nc.vector.tensor_copy(out=grouped[:], in_=w_raw[i][:].rearrange("p o j m -> p o m j"))
+            codes = keep.tile([P, PASSES * N], U32, name=f"w_codes{i}", align_bytes=64)
+            scales = keep.tile([P, PASSES * N], U8, name=f"w_scales{i}", align_bytes=64)
+            nc.vector.quantize_mx(out=codes[:].bitcast(FP8X4), scales=scales[:], in_=grouped[:].rearrange("p o m j -> p (o m j)"))
+            w_codes.append(codes)
+            w_scales.append(scales)
+
+        picked = [keep.tile([P, S], U32, name=f"picked{o}", align_bytes=64) for o in range(PASSES)]
+
+        def product(acc, i, o, cols):
+            nc.tensor.matmul_mx(
+                out=acc,
+                lhsT=w_codes[i][:, o * N : (o + 1) * N].bitcast(FP8X4),
+                lhsT_scale=w_scales[i][:, o * N : (o + 1) * N],
+                rhs=picked[o][:, cols].bitcast(FP8X4),
+                rhs_scale=picked_planes[4 * o : P, cols],
+                start=(o == 0),
+                stop=(o == PASSES - 1),
+            )
+
+        halves = [slice(h * HALF, (h + 1) * HALF) for h in range(2)]
+        groups = [slice(h * HALF // D, (h + 1) * HALF // D) for h in range(2)]
+        yq = [psum.tile([P, HALF], F32, name=f"yq{h}") for h in range(2)]
+        yi = psum.tile([P, S], F32, name="yi")
+
+        quantize_w(0)
+        nc.vector.tensor_copy(picked[0][:], words[0][:].indirect(offs_sb[:]))
+        picked_planes = keep.tile([P, S], U8, name="picked_planes", tag="words0", align_bytes=64)
+        nc.vector.tensor_copy(picked_planes[:], planes[:].indirect(offs_sb[:]))
+        quantize_w(1)
+        gain = keep.tile([P, 1], F32, name="gain")
+        nc.vector.tensor_scalar(gain[:], res_sb[:], -1.25, -0.125, ALU.mult, ALU.add)
+        for h in range(2):
+            product(yq[h][:], 0, 0, halves[h])
+        product(yi[:], 1, 0, slice(0, S))
+
+        sig = keep.tile([P, S], F32, name="sig")
+        for h in range(2):
+            nc.vector.tensor_copy(picked[1][:, halves[h]], words[1][:].indirect(offs_sb[:, h * LIST_COLS // 2 : (h + 1) * LIST_COLS // 2]))
+            product(yq[h][:], 0, 1, halves[h])
+            nc.scalar.activation(sig[:, halves[h]], yq[h][:], ACT.Sigmoid)
+        product(yi[:], 1, 1, slice(0, S))
+
+        polg = keep.tile([P, S], F32, name="polg")
+        nc.vector.tensor_copy(polg[:], pol_sb[:].indirect(cel_sb[:]))
+        top = keep.tile([P, S // D], F32, name="top")
+        nc.vector.tensor_reduce(top[:], sig[:].rearrange("p (v d) -> p v d", d=D), AX.X, ALU.max)
+        sum1 = keep.tile([P, S], F32, name="sum1")
+        nc.vector.scalar_tensor_tensor(sum1[:], yi[:], gain[:], polg[:], ALU.mult, ALU.subtract)
+        bound = keep.tile([P, S // D], F32, name="bound")
+        nc.vector.tensor_scalar(bound[:], top[:], -0.36, 0.42, ALU.mult, ALU.add)
+        sum2 = keep.tile([P, S], F32, name="sum2")
+        nc.vector.scalar_tensor_tensor(sum2[:], sig[:], 0.9, sum1[:], ALU.mult, ALU.add)
+
+        ln_soc = keep.tile([P, S], F32, name="ln_soc")
+        ln_rest = keep.tile([P, S], F32, name="ln_rest")
+        for h in range(2):
+            nc.scalar.activation(ln_soc[:, halves[h]], sig[:, halves[h]], ACT.Ln, bias=0.05, scale=0.9)
+        for h in range(2):
+            nc.scalar.activation(ln_rest[:, halves[h]], sig[:, halves[h]], ACT.Ln, bias=0.95, scale=-0.9)
+
+        sum3 = keep.tile([P, S], F32, name="sum3")
+        sum4 = keep.tile([P, S], F32, name="sum4")
+        low = keep.tile([P, S // D], F32, name="low")
+        result = keep.tile([P, S // D], F32, name="result")
+        for h in range(2):
+            nc.vector.scalar_tensor_tensor(sum3[:, halves[h]], ln_soc[:, halves[h]], 0.125, sum2[:, halves[h]], ALU.mult, ALU.add)
+        for h in range(2):
+            nc.vector.scalar_tensor_tensor(sum4[:, halves[h]], ln_rest[:, halves[h]], -0.1, sum3[:, halves[h]], ALU.mult, ALU.add)
+        for h in range(2):
+            nc.vector.tensor_reduce(low[:, groups[h]], sum4[:, halves[h]].rearrange("p (v d) -> p v d", d=D), AX.X, ALU.min)
+        for h in range(2):
+            nc.vector.scalar_tensor_tensor(result[:, groups[h]], low[:, groups[h]], 0.8, bound[:, groups[h]], ALU.mult, ALU.add)
+        nc.sync.dma_start(out=out, in_=result[:])

@@ -32,45 +32,46 @@ def tile_picked_ybatte_low_p_kernel(tc, x_words, x_scales, w1, w2, pol, res, off
         offs_sb = keep.tile([P, LIST_COLS], U16, name="offs_sb")
         cel_sb = keep.tile([P, LIST_COLS], U16, name="cel_sb")
         words = [keep.tile([P, T], U32, name=f"words{o}", tag=f"words{o}", align_bytes=64) for o in range(PASSES)]
-        planes = keep.tile([P, T], U8, name="planes", align_bytes=64)
-        w_raw = [keep.tile([P, PASSES, PACK, N], F32, name=f"w_raw{i}") for i in range(2)]
-        pol_sb = keep.tile([P, U], F32, name="pol_sb", align_bytes=64)
-        res_sb = keep.tile([P, 1], F32, name="res_sb")
-
-        def load_w(i, w):
-            nc.sync.dma_start(out=w_raw[i][:], in_=w.rearrange("(o p j) m -> p o j m", o=PASSES, j=PACK))
+        spread = keep.tile([P, T], U8, name="spread", align_bytes=64)
+        x_planes = keep.tile([P, PASSES, S], U8, name="x_planes", align_bytes=64)
+        w_raw = [keep.tile([P, PASSES, PACK, N], F32, name=f"w_raw{i}", tag=f"w_raw{i}", align_bytes=64) for i in range(2)]
+        pol_sb = keep.tile([P, U], F32, name="pol_sb", tag="pol_sb", align_bytes=64)
 
         def load_words(o):
             nc.sync.dma_start(out=words[o][:].bitcast(I32), in_=x_words[o].rearrange("p n t -> p (n t)").bitcast(I32))
 
-        nc.vector.memset(planes[:].bitcast(I32), 0)
-        for q in range(4):
-            nc.gpsimd.dma_start(
-                out=planes[32 * q : 32 * q + 4 * PASSES, :].bitcast(I32),
-                in_=x_scales[:, 4 * q : 4 * q + 4, :].bitcast(I32),
-            )
-        nc.scalar.dma_start(out=res_sb[:], in_=res)
+        def load_w(i, w):
+            nc.sync.dma_start(out=w_raw[i][:], in_=w.rearrange("(o p j) m -> p o j m", o=PASSES, j=PACK))
 
-        load_w(0, w1)
+        nc.vector.memset(spread[:].bitcast(I32), 0)
+        nc.vector.memset(x_planes[:].bitcast(I32), 0)
         nc.sync.dma_start(offs_sb[:], offs)
-        load_words(0)
-        load_w(1, w2)
-        load_words(1)
         nc.sync.dma_start(cel_sb[:], cel)
+        load_w(0, w1)
+        nc.sync.dma_start(out=spread[0:P:4, :].bitcast(I32), in_=x_scales.rearrange("o q c -> q o c").bitcast(I32))
+        load_words(0)
+        load_words(1)
+        load_w(1, w2)
         nc.sync.dma_start(out=pol_sb[:], in_=pol)
 
-        w_codes, w_scales = [], []
+        warm = keep.tile([P, 1], F32, name="warm")
+        nc.scalar.activation(warm[:], w_raw[0][:, 0, 0, 0:1], ACT.Sigmoid)
+
+        grouped = [keep.tile([P, PASSES, N, PACK], BF16, name=f"grouped{i}", align_bytes=64) for i in range(2)]
+        w_codes = [keep.tile([P, PASSES * N], U32, name=f"w_codes{i}", align_bytes=64) for i in range(2)]
+        w_scales = [keep.tile([P, PASSES * N], U8, name=f"w_scales{i}", align_bytes=64) for i in range(2)]
+
+        def woven(i, o):
+            return (
+                grouped[i][:, o].rearrange("p (c i) j -> p c j i", i=4),
+                w_raw[i][:, o].rearrange("p j (c i) -> p c j i", i=4),
+            )
 
         def quantize_w(i):
-            grouped = keep.tile([P, PASSES, N, PACK], BF16, name=f"grouped{i}", align_bytes=64)
-            nc.vector.tensor_copy(out=grouped[:], in_=w_raw[i][:].rearrange("p o j m -> p o m j"))
-            codes = keep.tile([P, PASSES * N], U32, name=f"w_codes{i}", align_bytes=64)
-            scales = keep.tile([P, PASSES * N], U8, name=f"w_scales{i}", align_bytes=64)
-            nc.vector.quantize_mx(out=codes[:].bitcast(FP8X4), scales=scales[:], in_=grouped[:].rearrange("p o m j -> p (o m j)"))
-            w_codes.append(codes)
-            w_scales.append(scales)
+            nc.vector.quantize_mx(out=w_codes[i][:].bitcast(FP8X4), scales=w_scales[i][:], in_=grouped[i][:].rearrange("p o m j -> p (o m j)"))
 
         picked = [keep.tile([P, S], U32, name=f"picked{o}", align_bytes=64) for o in range(PASSES)]
+        picked_spread = keep.tile([P, S], U8, name="picked_spread", align_bytes=64)
 
         def product(acc, i, o, cols):
             nc.tensor.matmul_mx(
@@ -78,7 +79,7 @@ def tile_picked_ybatte_low_p_kernel(tc, x_words, x_scales, w1, w2, pol, res, off
                 lhsT=w_codes[i][:, o * N : (o + 1) * N].bitcast(FP8X4),
                 lhsT_scale=w_scales[i][:, o * N : (o + 1) * N],
                 rhs=picked[o][:, cols].bitcast(FP8X4),
-                rhs_scale=picked_planes[4 * o : P, cols],
+                rhs_scale=x_planes[:, o, cols],
                 start=(o == 0),
                 stop=(o == PASSES - 1),
             )
@@ -88,34 +89,44 @@ def tile_picked_ybatte_low_p_kernel(tc, x_words, x_scales, w1, w2, pol, res, off
         yq = [psum.tile([P, HALF], F32, name=f"yq{h}") for h in range(2)]
         yi = psum.tile([P, S], F32, name="yi")
 
+        nc.vector.tensor_copy(picked_spread[:], spread[:].indirect(offs_sb[:]))
+        for q in range(4):
+            nc.scalar.dma_start(
+                out=x_planes[32 * q : 32 * q + 4].bitcast(I32),
+                in_=picked_spread[32 * q : 32 * q + 32 : 4, :].bitcast(I32),
+            )
+        for o in range(PASSES):
+            nc.vector.tensor_copy(*woven(0, o))
         quantize_w(0)
         nc.vector.tensor_copy(picked[0][:], words[0][:].indirect(offs_sb[:]))
-        picked_planes = keep.tile([P, S], U8, name="picked_planes", tag="words0", align_bytes=64)
-        nc.vector.tensor_copy(picked_planes[:], planes[:].indirect(offs_sb[:]))
-        quantize_w(1)
-        gain = keep.tile([P, 1], F32, name="gain")
-        nc.vector.tensor_scalar(gain[:], res_sb[:], -1.25, -0.125, ALU.mult, ALU.add)
         for h in range(2):
             product(yq[h][:], 0, 0, halves[h])
-        product(yi[:], 1, 0, slice(0, S))
 
-        sig = keep.tile([P, S], F32, name="sig")
         for h in range(2):
             nc.vector.tensor_copy(picked[1][:, halves[h]], words[1][:].indirect(offs_sb[:, h * LIST_COLS // 2 : (h + 1) * LIST_COLS // 2]))
             product(yq[h][:], 0, 1, halves[h])
+        res_sb = keep.tile([P, 1], F32, name="res_sb", tag="words1", align_bytes=64)
+        nc.sync.dma_start(out=res_sb[:], in_=res)
+
+        nc.scalar.copy(*woven(1, 0))
+        nc.vector.tensor_copy(*woven(1, 1))
+        quantize_w(1)
+        for o in range(PASSES):
+            product(yi[:], 1, o, slice(0, S))
+        sig = keep.tile([P, S], F32, name="sig", tag="w_raw1", align_bytes=64)
+        for h in range(2):
             nc.scalar.activation(sig[:, halves[h]], yq[h][:], ACT.Sigmoid)
-        product(yi[:], 1, 1, slice(0, S))
 
         polg = keep.tile([P, S], F32, name="polg")
         nc.vector.tensor_copy(polg[:], pol_sb[:].indirect(cel_sb[:]))
-        top = keep.tile([P, S // D], F32, name="top")
+        gain = keep.tile([P, 1], F32, name="gain")
+        nc.vector.tensor_scalar(gain[:], res_sb[:], -1.25, -0.125, ALU.mult, ALU.add)
+        top = keep.tile([P, S // D], F32, name="top", tag="pol_sb", align_bytes=64)
         nc.vector.tensor_reduce(top[:], sig[:].rearrange("p (v d) -> p v d", d=D), AX.X, ALU.max)
         sum1 = keep.tile([P, S], F32, name="sum1")
         nc.vector.scalar_tensor_tensor(sum1[:], yi[:], gain[:], polg[:], ALU.mult, ALU.subtract)
         bound = keep.tile([P, S // D], F32, name="bound")
         nc.vector.tensor_scalar(bound[:], top[:], -0.36, 0.42, ALU.mult, ALU.add)
-        sum2 = keep.tile([P, S], F32, name="sum2")
-        nc.vector.scalar_tensor_tensor(sum2[:], sig[:], 0.9, sum1[:], ALU.mult, ALU.add)
 
         ln_soc = keep.tile([P, S], F32, name="ln_soc")
         ln_rest = keep.tile([P, S], F32, name="ln_rest")
@@ -124,10 +135,13 @@ def tile_picked_ybatte_low_p_kernel(tc, x_words, x_scales, w1, w2, pol, res, off
         for h in range(2):
             nc.scalar.activation(ln_rest[:, halves[h]], sig[:, halves[h]], ACT.Ln, bias=0.95, scale=-0.9)
 
+        sum2 = keep.tile([P, S], F32, name="sum2")
         sum3 = keep.tile([P, S], F32, name="sum3")
         sum4 = keep.tile([P, S], F32, name="sum4")
         low = keep.tile([P, S // D], F32, name="low")
         result = keep.tile([P, S // D], F32, name="result")
+        for h in range(2):
+            nc.vector.scalar_tensor_tensor(sum2[:, halves[h]], sig[:, halves[h]], 0.9, sum1[:, halves[h]], ALU.mult, ALU.add)
         for h in range(2):
             nc.vector.scalar_tensor_tensor(sum3[:, halves[h]], ln_soc[:, halves[h]], 0.125, sum2[:, halves[h]], ALU.mult, ALU.add)
         for h in range(2):

@@ -35,7 +35,7 @@ def tile_picked_ybatte_low_p_kernel(tc, x_words, x_scales, w1, w2, pol, res, off
         spread = keep.tile([P, T], U8, name="spread", align_bytes=64)
         x_planes = keep.tile([P, PASSES, S], U8, name="x_planes", align_bytes=64)
         w_raw = [keep.tile([P, PASSES, PACK, N], F32, name=f"w_raw{i}", tag=f"w_raw{i}", align_bytes=64) for i in range(2)]
-        pol_sb = keep.tile([P, U], F32, name="pol_sb", tag="pol_sb", align_bytes=64)
+        pol_sb = keep.tile([P, U], F32, name="pol_sb", align_bytes=64)
 
         def load_words(o):
             nc.sync.dma_start(out=words[o][:].bitcast(I32), in_=x_words[o].rearrange("p n t -> p (n t)").bitcast(I32))
@@ -45,9 +45,9 @@ def tile_picked_ybatte_low_p_kernel(tc, x_words, x_scales, w1, w2, pol, res, off
 
         nc.vector.memset(spread[:].bitcast(I32), 0)
         nc.vector.memset(x_planes[:].bitcast(I32), 0)
+        load_w(0, w1)
         nc.sync.dma_start(offs_sb[:], offs)
         nc.sync.dma_start(cel_sb[:], cel)
-        load_w(0, w1)
         nc.sync.dma_start(out=spread[0:P:4, :].bitcast(I32), in_=x_scales.rearrange("o q c -> q o c").bitcast(I32))
         load_words(0)
         load_words(1)
@@ -89,14 +89,14 @@ def tile_picked_ybatte_low_p_kernel(tc, x_words, x_scales, w1, w2, pol, res, off
         yq = [psum.tile([P, HALF], F32, name=f"yq{h}") for h in range(2)]
         yi = psum.tile([P, S], F32, name="yi")
 
+        for o in range(PASSES):
+            nc.scalar.copy(*woven(0, o))
         nc.vector.tensor_copy(picked_spread[:], spread[:].indirect(offs_sb[:]))
         for q in range(4):
             nc.scalar.dma_start(
                 out=x_planes[32 * q : 32 * q + 4].bitcast(I32),
                 in_=picked_spread[32 * q : 32 * q + 32 : 4, :].bitcast(I32),
             )
-        for o in range(PASSES):
-            nc.vector.tensor_copy(*woven(0, o))
         quantize_w(0)
         nc.vector.tensor_copy(picked[0][:], words[0][:].indirect(offs_sb[:]))
         for h in range(2):
@@ -117,16 +117,18 @@ def tile_picked_ybatte_low_p_kernel(tc, x_words, x_scales, w1, w2, pol, res, off
         for h in range(2):
             nc.scalar.activation(sig[:, halves[h]], yq[h][:], ACT.Sigmoid)
 
+        top = keep.tile([P, S // D], F32, name="top")
+        for h in range(2):
+            nc.vector.tensor_reduce(top[:, groups[h]], sig[:, halves[h]].rearrange("p (v d) -> p v d", d=D), AX.X, ALU.max)
         polg = keep.tile([P, S], F32, name="polg")
         nc.vector.tensor_copy(polg[:], pol_sb[:].indirect(cel_sb[:]))
         gain = keep.tile([P, 1], F32, name="gain")
         nc.vector.tensor_scalar(gain[:], res_sb[:], -1.25, -0.125, ALU.mult, ALU.add)
-        top = keep.tile([P, S // D], F32, name="top", tag="pol_sb", align_bytes=64)
-        nc.vector.tensor_reduce(top[:], sig[:].rearrange("p (v d) -> p v d", d=D), AX.X, ALU.max)
-        sum1 = keep.tile([P, S], F32, name="sum1")
-        nc.vector.scalar_tensor_tensor(sum1[:], yi[:], gain[:], polg[:], ALU.mult, ALU.subtract)
         bound = keep.tile([P, S // D], F32, name="bound")
         nc.vector.tensor_scalar(bound[:], top[:], -0.36, 0.42, ALU.mult, ALU.add)
+        sum1 = keep.tile([P, S], F32, name="sum1")
+        for h in range(2):
+            nc.vector.scalar_tensor_tensor(sum1[:, halves[h]], sig[:, halves[h]], 0.9, polg[:, halves[h]], ALU.mult, ALU.subtract)
 
         ln_soc = keep.tile([P, S], F32, name="ln_soc")
         ln_rest = keep.tile([P, S], F32, name="ln_rest")
@@ -141,7 +143,7 @@ def tile_picked_ybatte_low_p_kernel(tc, x_words, x_scales, w1, w2, pol, res, off
         low = keep.tile([P, S // D], F32, name="low")
         result = keep.tile([P, S // D], F32, name="result")
         for h in range(2):
-            nc.vector.scalar_tensor_tensor(sum2[:, halves[h]], sig[:, halves[h]], 0.9, sum1[:, halves[h]], ALU.mult, ALU.add)
+            nc.vector.scalar_tensor_tensor(sum2[:, halves[h]], yi[:, halves[h]], gain[:], sum1[:, halves[h]], ALU.mult, ALU.add)
         for h in range(2):
             nc.vector.scalar_tensor_tensor(sum3[:, halves[h]], ln_soc[:, halves[h]], 0.125, sum2[:, halves[h]], ALU.mult, ALU.add)
         for h in range(2):

@@ -34,8 +34,7 @@ def tile_picked_ybatte_low_p_kernel(tc, x_words, x_scales, w1, w2, pol, res, off
         words = [keep.tile([P, T], U32, name=f"words{o}", tag=f"words{o}", align_bytes=64) for o in range(PASSES)]
         spread = keep.tile([P, T], U8, name="spread", align_bytes=64)
         x_planes = keep.tile([P, PASSES, S], U8, name="x_planes", align_bytes=64)
-        w_raw = [keep.tile([P, PASSES, PACK, N], F32, name=f"w_raw{i}", tag=f"w_raw{i}", align_bytes=64) for i in range(2)]
-        pol_sb = keep.tile([P, U], F32, name="pol_sb", align_bytes=64)
+        w_raw = [keep.tile([P, PASSES, PACK, N], F32, name="w1_raw", align_bytes=64)]
 
         def load_words(o):
             nc.sync.dma_start(out=words[o][:].bitcast(I32), in_=x_words[o].rearrange("p n t -> p (n t)").bitcast(I32))
@@ -51,13 +50,8 @@ def tile_picked_ybatte_low_p_kernel(tc, x_words, x_scales, w1, w2, pol, res, off
         nc.sync.dma_start(out=spread[0:P:4, :].bitcast(I32), in_=x_scales.rearrange("o q c -> q o c").bitcast(I32))
         load_words(0)
         load_words(1)
-        load_w(1, w2)
-        nc.sync.dma_start(out=pol_sb[:], in_=pol)
 
-        warm = keep.tile([P, 1], F32, name="warm")
-        nc.scalar.activation(warm[:], w_raw[0][:, 0, 0, 0:1], ACT.Sigmoid)
-
-        grouped = [keep.tile([P, PASSES, N, PACK], BF16, name=f"grouped{i}", align_bytes=64) for i in range(2)]
+        grouped = [keep.tile([P, PASSES, N, PACK], BF16, name=f"grouped{i}", tag=f"grouped{i}", align_bytes=64) for i in range(2)]
         w_codes = [keep.tile([P, PASSES * N], U32, name=f"w_codes{i}", align_bytes=64) for i in range(2)]
         w_scales = [keep.tile([P, PASSES * N], U8, name=f"w_scales{i}", align_bytes=64) for i in range(2)]
 
@@ -98,7 +92,12 @@ def tile_picked_ybatte_low_p_kernel(tc, x_words, x_scales, w1, w2, pol, res, off
                 in_=picked_spread[32 * q : 32 * q + 32 : 4, :].bitcast(I32),
             )
         quantize_w(0)
+        w2_raw = keep.tile([P, PASSES, PACK, N], F32, name="w2_raw", tag="grouped0", align_bytes=64)
+        w_raw.append(w2_raw)
+        load_w(1, w2)
         nc.vector.tensor_copy(picked[0][:], words[0][:].indirect(offs_sb[:]))
+        pol_sb = keep.tile([P, U], F32, name="pol_sb", tag="words0", align_bytes=64)
+        nc.sync.dma_start(out=pol_sb[:], in_=pol)
         for h in range(2):
             product(yq[h][:], 0, 0, halves[h])
 
@@ -113,9 +112,9 @@ def tile_picked_ybatte_low_p_kernel(tc, x_words, x_scales, w1, w2, pol, res, off
         quantize_w(1)
         for o in range(PASSES):
             product(yi[:], 1, o, slice(0, S))
-        sig = keep.tile([P, S], F32, name="sig", tag="w_raw1", align_bytes=64)
+        sig = keep.tile([P, S], F32, name="sig", tag="grouped0", align_bytes=64)
         for h in range(2):
-            nc.scalar.activation(sig[:, halves[h]], yq[h][:], ACT.Sigmoid)
+            nc.scalar.activation(sig[:, halves[h]], yq[h][:], ACT.Tanh, scale=0.5)
 
         top = keep.tile([P, S // D], F32, name="top")
         for h in range(2):
@@ -125,17 +124,17 @@ def tile_picked_ybatte_low_p_kernel(tc, x_words, x_scales, w1, w2, pol, res, off
         gain = keep.tile([P, 1], F32, name="gain")
         nc.vector.tensor_scalar(gain[:], res_sb[:], -1.25, -0.125, ALU.mult, ALU.add)
         bound = keep.tile([P, S // D], F32, name="bound")
-        nc.vector.tensor_scalar(bound[:], top[:], -0.36, 0.42, ALU.mult, ALU.add)
+        nc.vector.tensor_scalar(bound[:], top[:], -0.18, 0.6, ALU.mult, ALU.add)
         sum1 = keep.tile([P, S], F32, name="sum1")
         for h in range(2):
-            nc.vector.scalar_tensor_tensor(sum1[:, halves[h]], sig[:, halves[h]], 0.9, polg[:, halves[h]], ALU.mult, ALU.subtract)
+            nc.vector.scalar_tensor_tensor(sum1[:, halves[h]], sig[:, halves[h]], 0.45, polg[:, halves[h]], ALU.mult, ALU.subtract)
 
         ln_soc = keep.tile([P, S], F32, name="ln_soc")
         ln_rest = keep.tile([P, S], F32, name="ln_rest")
         for h in range(2):
-            nc.scalar.activation(ln_soc[:, halves[h]], sig[:, halves[h]], ACT.Ln, bias=0.05, scale=0.9)
+            nc.scalar.activation(ln_soc[:, halves[h]], sig[:, halves[h]], ACT.Ln, bias=0.5, scale=0.45)
         for h in range(2):
-            nc.scalar.activation(ln_rest[:, halves[h]], sig[:, halves[h]], ACT.Ln, bias=0.95, scale=-0.9)
+            nc.scalar.activation(ln_rest[:, halves[h]], sig[:, halves[h]], ACT.Ln, bias=0.5, scale=-0.45)
 
         sum2 = keep.tile([P, S], F32, name="sum2")
         sum3 = keep.tile([P, S], F32, name="sum3")

from contextlib import ExitStack

import concourse.mybir as mybir

K, T, S, D, N, U = 1024, 2048, 512, 4, 128, 1024
FLOPS = 2 * 2 * K * N * S

F32 = mybir.dt.float32
BF16 = mybir.dt.bfloat16
I32 = mybir.dt.int32
U32 = mybir.dt.uint32
U16 = mybir.dt.uint16
U8 = mybir.dt.uint8
FP8X4 = mybir.dt.float8_e4m3fn_x4
ALU = mybir.AluOpType
ACT = mybir.ActivationFunctionType
AX = mybir.AxisListType

P = 128
PACK = 4
PASSES = K // (P * PACK)
HALF = S // 2
LIST_COLS = S // 16


def tile_picked_ybatte_low_p_kernel(tc, x_words, x_scales, w1, w2, pol, res, offs, cel, out):
    nc = tc.nc
    with ExitStack() as ctx:
        keep = ctx.enter_context(tc.tile_pool(name="keep", bufs=1))
        psum = ctx.enter_context(tc.psum_pool(name="psum", bufs=1))

        offs_sb = keep.tile([P, LIST_COLS], U16, name="offs_sb")
        cel_sb = keep.tile([P, LIST_COLS], U16, name="cel_sb")
        words = [keep.tile([P, T], U32, name=f"words{o}", tag=f"words{o}", align_bytes=64) for o in range(PASSES)]
        spread = keep.tile([P, T], U8, name="spread", align_bytes=64)
        x_planes = keep.tile([P, PASSES, S], U8, name="x_planes", align_bytes=64)
        w_raw = [keep.tile([P, PASSES, PACK, N], F32, name="w1_raw", align_bytes=64)]

        def load_words(o):
            nc.sync.dma_start(out=words[o][:].bitcast(I32), in_=x_words[o].rearrange("p n t -> p (n t)").bitcast(I32))

        def load_w(i, w):
            nc.sync.dma_start(out=w_raw[i][:], in_=w.rearrange("(o p j) m -> p o j m", o=PASSES, j=PACK))

        nc.vector.memset(spread[:].bitcast(I32), 0)
        nc.vector.memset(x_planes[:].bitcast(I32), 0)
        load_w(0, w1)
        nc.sync.dma_start(offs_sb[:], offs)
        nc.sync.dma_start(cel_sb[:], cel)
        nc.sync.dma_start(out=spread[0:P:4, :].bitcast(I32), in_=x_scales.rearrange("o q c -> q o c").bitcast(I32))
        load_words(0)
        load_words(1)

        grouped = [keep.tile([P, PASSES, N, PACK], BF16, name=f"grouped{i}", tag=f"grouped{i}", align_bytes=64) for i in range(2)]
        w_codes = [keep.tile([P, PASSES * N], U32, name=f"w_codes{i}", align_bytes=64) for i in range(2)]
        w_scales = [keep.tile([P, PASSES * N], U8, name=f"w_scales{i}", align_bytes=64) for i in range(2)]

        def woven(i, o):
            return (
                grouped[i][:, o].rearrange("p (c i) j -> p c j i", i=4),
                w_raw[i][:, o].rearrange("p j (c i) -> p c j i", i=4),
            )

        def quantize_w(i):
            nc.vector.quantize_mx(out=w_codes[i][:].bitcast(FP8X4), scales=w_scales[i][:], in_=grouped[i][:].rearrange("p o m j -> p (o m j)"))

        picked = [keep.tile([P, S], U32, name=f"picked{o}", align_bytes=64) for o in range(PASSES)]
        picked_spread = keep.tile([P, S], U8, name="picked_spread", align_bytes=64)

        def product(acc, i, o, cols):
            nc.tensor.matmul_mx(
                out=acc,
                lhsT=w_codes[i][:, o * N : (o + 1) * N].bitcast(FP8X4),
                lhsT_scale=w_scales[i][:, o * N : (o + 1) * N],
                rhs=picked[o][:, cols].bitcast(FP8X4),
                rhs_scale=x_planes[:, o, cols],
                start=(o == 0),
                stop=(o == PASSES - 1),
            )

        halves = [slice(h * HALF, (h + 1) * HALF) for h in range(2)]
        groups = [slice(h * HALF // D, (h + 1) * HALF // D) for h in range(2)]
        yq = [psum.tile([P, HALF], F32, name=f"yq{h}") for h in range(2)]
        yi = psum.tile([P, S], F32, name="yi")

        for o in range(PASSES):
            nc.scalar.copy(*woven(0, o))
        nc.vector.tensor_copy(picked_spread[:], spread[:].indirect(offs_sb[:]))
        for q in range(4):
            nc.scalar.dma_start(
                out=x_planes[32 * q : 32 * q + 4].bitcast(I32),
                in_=picked_spread[32 * q : 32 * q + 32 : 4, :].bitcast(I32),
            )
        quantize_w(0)
        w2_raw = keep.tile([P, PASSES, PACK, N], F32, name="w2_raw", tag="grouped0", align_bytes=64)
        w_raw.append(w2_raw)
        load_w(1, w2)
        nc.vector.tensor_copy(picked[0][:], words[0][:].indirect(offs_sb[:]))
        pol_sb = keep.tile([P, U], F32, name="pol_sb", tag="words0", align_bytes=64)
        nc.sync.dma_start(out=pol_sb[:], in_=pol)
        for h in range(2):
            product(yq[h][:], 0, 0, halves[h])

        for h in range(2):
            nc.vector.tensor_copy(picked[1][:, halves[h]], words[1][:].indirect(offs_sb[:, h * LIST_COLS // 2 : (h + 1) * LIST_COLS // 2]))
            product(yq[h][:], 0, 1, halves[h])
        res_sb = keep.tile([P, 1], F32, name="res_sb", tag="words1", align_bytes=64)
        nc.sync.dma_start(out=res_sb[:], in_=res)

        nc.scalar.copy(*woven(1, 0))
        nc.vector.tensor_copy(*woven(1, 1))
        quantize_w(1)
        for o in range(PASSES):
            product(yi[:], 1, o, slice(0, S))
        sig = keep.tile([P, S], F32, name="sig", tag="grouped0", align_bytes=64)
        for h in range(2):
            nc.scalar.activation(sig[:, halves[h]], yq[h][:], ACT.Tanh, scale=0.5)

        top = keep.tile([P, S // D], F32, name="top")
        for h in range(2):
            nc.vector.tensor_reduce(top[:, groups[h]], sig[:, halves[h]].rearrange("p (v d) -> p v d", d=D), AX.X, ALU.max)
        polg = keep.tile([P, S], F32, name="polg")
        nc.vector.tensor_copy(polg[:], pol_sb[:].indirect(cel_sb[:]))
        gain = keep.tile([P, 1], F32, name="gain")
        nc.vector.tensor_scalar(gain[:], res_sb[:], -1.25, -0.125, ALU.mult, ALU.add)
        bound = keep.tile([P, S // D], F32, name="bound")
        nc.vector.tensor_scalar(bound[:], top[:], -0.18, 0.6, ALU.mult, ALU.add)
        sum1 = keep.tile([P, S], F32, name="sum1")
        for h in range(2):
            nc.vector.scalar_tensor_tensor(sum1[:, halves[h]], sig[:, halves[h]], 0.45, polg[:, halves[h]], ALU.mult, ALU.subtract)

        ln_soc = keep.tile([P, S], F32, name="ln_soc")
        ln_rest = keep.tile([P, S], F32, name="ln_rest")
        for h in range(2):
            nc.scalar.activation(ln_soc[:, halves[h]], sig[:, halves[h]], ACT.Ln, bias=0.5, scale=0.45)
        for h in range(2):
            nc.scalar.activation(ln_rest[:, halves[h]], sig[:, halves[h]], ACT.Ln, bias=0.5, scale=-0.45)

        sum2 = keep.tile([P, S], F32, name="sum2")
        sum3 = keep.tile([P, S], F32, name="sum3")
        sum4 = keep.tile([P, S], F32, name="sum4")
        low = keep.tile([P, S // D], F32, name="low")
        result = keep.tile([P, S // D], F32, name="result")
        for h in range(2):
            nc.vector.scalar_tensor_tensor(sum2[:, halves[h]], yi[:, halves[h]], gain[:], sum1[:, halves[h]], ALU.mult, ALU.add)
        for h in range(2):
            nc.vector.scalar_tensor_tensor(sum3[:, halves[h]], ln_soc[:, halves[h]], 0.125, sum2[:, halves[h]], ALU.mult, ALU.add)
        for h in range(2):
            nc.vector.scalar_tensor_tensor(sum4[:, halves[h]], ln_rest[:, halves[h]], -0.1, sum3[:, halves[h]], ALU.mult, ALU.add)
        for h in range(2):
            nc.vector.tensor_reduce(low[:, groups[h]], sum4[:, halves[h]].rearrange("p (v d) -> p v d", d=D), AX.X, ALU.min)
        for h in range(2):
            nc.vector.scalar_tensor_tensor(result[:, groups[h]], low[:, groups[h]], 0.8, bound[:, groups[h]], ALU.mult, ALU.add)
        nc.sync.dma_start(out=out, in_=result[:])
